import numpy as np, ml_dtypes
CORES = [34,162,290,418,42,426]
N = 6
WB, KB, QP = 3, 1, 512
def setup_inputs(rng):
    return {"q": rng.standard_normal((N, 128, QP), dtype=np.float32).astype(ml_dtypes.bfloat16), "k": rng.standard_normal((N, 128, KB * 128), dtype=np.float32).astype(ml_dtypes.bfloat16), "v": rng.standard_normal((N, 128, KB * 128), dtype=np.float32).astype(ml_dtypes.bfloat16)}
def setup_inputs_big(rng):
    d = setup_inputs(rng)
    for k in ("q", "k", "v"): d[k] = (d[k].astype(np.float32) * 1024.0).astype(d[k].dtype)
    return d
def setup_inputs_small(rng):
    d = setup_inputs(rng)
    for k in ("q", "k", "v"): d[k] = (d[k].astype(np.float32) * (1 / 1024.0)).astype(d[k].dtype)
    return d
def setup_inputs_apart(rng):
    d = setup_inputs(rng)
    f = (10.0 ** rng.permutation(np.linspace(-1.5, 1.5, N))).astype(np.float32).reshape(N, 1, 1)
    for k in ("q", "k", "v"): d[k] = (d[k].astype(np.float32) * f).astype(d[k].dtype)
    return d
def reference(q, k, v):
    Q, K, V = q.astype(np.float64), k.astype(np.float64), v.astype(np.float64)
    y = np.zeros((N, 128, QP))
    for r in range(N):
        for j in range(max(0, r - WB), r + 1):
            for b in range(KB):
                S = np.maximum(K[j][:, 128 * b:128 * b + 128].T @ Q[r], 0.0)
                y[r] += V[j][:, 128 * b:128 * b + 128].T @ S
    return {"y": y.astype(ml_dtypes.bfloat16 if q.dtype != np.float64 else np.float64)}

@@ -1,0 +1,154 @@
+from concourse.bass import DstId, RemoteDMATransfer
+from concourse.mybir import AluOpType
+
+WB = 3
+SLOTS = WB + 1
+KP = 128
+QP = 512
+P = 2
+W = QP // P
+NS = 8 - P
+ST = 2
+
+SCRATCH = {
+    "qs": ("sbuf", [128, QP], "bfloat16"),
+    "zero": ("sbuf", [128, W], "float32"),
+    "ys": ("sbuf", [128, QP], "bfloat16"),
+}
+for _s in range(SLOTS):
+    SCRATCH["kv%d" % _s] = ("sbuf", [128, 2 * KP], "bfloat16")
+for _t in range(SLOTS * P):
+    SCRATCH["s%d" % _t] = ("sbuf", [128, W], "bfloat16")
+for _h in range(P):
+    SCRATCH["o%d" % _h] = ("psum", [128, 512], "float32")
+for _b in range(NS):
+    SCRATCH["p%d" % _b] = ("psum", [128, 512], "float32")
+
+SEMAPHORES = (["kvl", "ql", "zs", "sent", "st"] + ["a%d" % s for s in range(SLOTS)]
+              + ["m%d" % t for t in range(SLOTS * P)] + ["r%d" % t for t in range(SLOTS * P)]
+              + ["f%d" % h for h in range(P)] + ["c%d" % h for h in range(P)])
+
+
+def _bits(m):
+    return bin(m).count("1")
+
+
+def _plan(cores, topo):
+    n = len(cores)
+    first = [[] for _ in range(n)]
+    rest = [[] for _ in range(n)]
+    relay = [[] for _ in range(n)]
+    for j in range(n):
+        dests = list(range(j + 1, min(j + WB, n - 1) + 1))
+        direct = [r for r in dests if topo.may_write(cores[j], cores[r])]
+        for r in dests:
+            if r in direct:
+                continue
+            cands = [m for m in direct if topo.may_write(cores[m], cores[r])]
+            m = min(cands, key=lambda x: (x >= n - 1, len(relay[x]), x))
+            relay[m].append((j, r))
+            if m not in first[j]:
+                first[j].append(m)
+        rest[j] = [r for r in direct if r not in first[j]]
+    calls = [[] for _ in range(n)]
+    due = [{r: (0, 0)} for r in range(n)]
+
+    def add(m, j, group, stage):
+        mask = topo.mask(cores[m], cores[group[0]])
+        for r in group[1:]:
+            mask &= topo.mask(cores[m], cores[r])
+        calls[m].append((j, group, mask))
+        for r in group:
+            due[r][j] = (stage, _bits(mask))
+
+    for j in range(n):
+        for r in first[j]:
+            add(j, j, [r], 1)
+        if rest[j]:
+            add(j, j, rest[j], 2)
+    for m in range(n):
+        for j, r in relay[m]:
+            add(m, j, [r], 3)
+    return calls, due
+
+
+def rank_program(g, core, T, topo):
+    rank = T.rank_of(core)
+    if rank is None:
+        return
+    cores = list(T.cores)
+    calls, due = _plan(cores, topo)
+    sem = T.sem
+    te, ve = g.tensor, g.vector
+
+    def slot(j):
+        return T["kv%d" % (j % SLOTS)]
+
+    def arr(j):
+        return sem["a%d" % (j % SLOTS)]
+
+    mine = slot(rank)
+    g.sync.dma_start(mine[:, 0:KP], T.k[:]).then_inc(sem.kvl, 16)
+    g.scalar.dma_start(mine[:, KP:2 * KP], T.v[:]).then_inc(sem.kvl, 16)
+    g.sync.dma_start(T.qs[:], T.q[:]).then_inc(sem.ql, 16)
+    ve.memset(T.zero[:], 0.0).then_inc(sem.zs, 1)
+
+    left = 0
+    if calls[rank]:
+        g.wait_ge(sem.kvl, 32)
+    for j, group, mask in calls[rank]:
+        if j != rank:
+            g.wait_ge(arr(j), due[rank][j][1])
+        buf = slot(j)
+        if len(group) == 1:
+            rid, pid = topo.addr(cores[group[0]], core)
+            g.remote_dma(buf[:], buf[:], arr(j), sem.sent, pid, rid, mask)
+        else:
+            ids = []
+            for r in group:
+                rid, pid = topo.addr(cores[r], core)
+                ids.append(DstId(rid=rid, pnc=pid))
+            g.remote_dma_fused([RemoteDMATransfer(dst_ids=ids, dma_engine_mask=mask, remote_sem=arr(j),
+                                                  srcs=[buf[:]], dsts=[buf[:] for _ in group], alu_op=0)],
+                               local_sem=sem.sent)
+        left += _bits(mask)
+
+    order = sorted(due[rank], key=lambda j: (due[rank][j][0], rank - j))
+    last = len(order) - 1
+    te.wait_ge(sem.ql, 16)
+    ve.wait_ge(sem.zs, 1)
+    for i, j in enumerate(order):
+        buf = slot(j)
+        if j == rank:
+            te.wait_ge(sem.kvl, 32)
+        else:
+            te.wait_ge(arr(j), due[rank][j][1])
+        for h in range(P):
+            t = i * P + h
+            bank = T["p%d" % (t % NS)]
+            te.matmul(bank[:, 0:W], buf[:, 0:KP], T.qs[:, h * W:(h + 1) * W],
+                      start=True, stop=True).then_inc(sem["m%d" % t], 1)
+            ve.wait_ge(sem["m%d" % t], 1)
+            ve.tensor_tensor(T["s%d" % t][:], bank[:, 0:W], T.zero[:], AluOpType.max).then_inc(sem["r%d" % t], 1)
+        for h in range(P):
+            t = i * P + h
+            te.wait_ge(sem["r%d" % t], 1)
+            mm = te.matmul(T["o%d" % h][:, 0:W], buf[:, KP:2 * KP], T["s%d" % t][:], start=(i == 0), stop=(i == last))
+            if i == last:
+                mm.then_inc(sem["f%d" % h], 1)
+    for h in range(P):
+        ve.wait_ge(sem["f%d" % h], 1)
+        ve.tensor_copy(T.ys[:, h * W:(h + 1) * W], T["o%d" % h][:, 0:W]).then_inc(sem["c%d" % h], 1)
+
+    queues = [g.sync, g.scalar]
+    per = P // ST
+    for s in range(ST):
+        qu = queues[s % 2]
+        for h in range(s * per, (s + 1) * per):
+            qu.wait_ge(sem["c%d" % h], 1)
+        lo, hi = s * per * W, (s + 1) * per * W
+        qu.dma_start(T.y[:, lo:hi], T.ys[:, lo:hi]).then_inc(sem.st, 16)
+
+    if left:
+        g.wait_ge(sem.sent, left)
+    g.wait_ge(sem.st, 16 * ST)

@@ -24,7 +24,7 @@ for _h in range(P):
 for _b in range(NS):
     SCRATCH["p%d" % _b] = ("psum", [128, 512], "float32")
 
-SEMAPHORES = (["kvl", "ql", "zs", "sent", "st"] + ["a%d" % s for s in range(SLOTS)]
+SEMAPHORES = (["kvl", "ql", "zs", "sent", "st"] + ["a%d" % s for s in range(SLOTS)] + ["b%d" % s for s in range(SLOTS)]
               + ["m%d" % t for t in range(SLOTS * P)] + ["r%d" % t for t in range(SLOTS * P)]
               + ["f%d" % h for h in range(P)] + ["c%d" % h for h in range(P)])
 
@@ -51,15 +51,20 @@ def _plan(cores, topo):
                 first[j].append(m)
         rest[j] = [r for r in direct if r not in first[j]]
     calls = [[] for _ in range(n)]
-    due = [{r: (0, 0)} for r in range(n)]
+    due = [{r: (0, 0, 1)} for r in range(n)]
 
     def add(m, j, group, stage):
         mask = topo.mask(cores[m], cores[group[0]])
         for r in group[1:]:
             mask &= topo.mask(cores[m], cores[r])
-        calls[m].append((j, group, mask))
+        parts = 1 if stage == 2 else 2
+        if parts == 1:
+            calls[m].append((j, group, mask, 0))
+        else:
+            calls[m].append((j, group, mask, 1))
+            calls[m].append((j, group, mask, 2))
         for r in group:
-            due[r][j] = (stage, _bits(mask))
+            due[r][j] = (stage, _bits(mask), parts)
 
     for j in range(n):
         for r in first[j]:
@@ -84,8 +89,8 @@ def rank_program(g, core, T, topo):
     def slot(j):
         return T["kv%d" % (j % SLOTS)]
 
-    def arr(j):
-        return sem["a%d" % (j % SLOTS)]
+    def arr(j, part=0):
+        return sem[("b%d" if part == 2 else "a%d") % (j % SLOTS)]
 
     mine = slot(rank)
     g.sync.dma_start(mine[:, 0:KP], T.k[:]).then_inc(sem.kvl, 16)
@@ -96,20 +101,21 @@ def rank_program(g, core, T, topo):
     left = 0
     if calls[rank]:
         g.wait_ge(sem.kvl, 32)
-    for j, group, mask in calls[rank]:
+    for j, group, mask, part in calls[rank]:
         if j != rank:
-            g.wait_ge(arr(j), due[rank][j][1])
-        buf = slot(j)
+            g.wait_ge(arr(j, part), due[rank][j][1])
+        lo, hi = [(0, 2 * KP), (0, KP), (KP, 2 * KP)][part]
+        piece = slot(j)[:, lo:hi]
         if len(group) == 1:
             rid, pid = topo.addr(cores[group[0]], core)
-            g.remote_dma(buf[:], buf[:], arr(j), sem.sent, pid, rid, mask)
+            g.remote_dma(piece, piece, arr(j, part), sem.sent, pid, rid, mask)
         else:
             ids = []
             for r in group:
                 rid, pid = topo.addr(cores[r], core)
                 ids.append(DstId(rid=rid, pnc=pid))
-            g.remote_dma_fused([RemoteDMATransfer(dst_ids=ids, dma_engine_mask=mask, remote_sem=arr(j),
-                                                  srcs=[buf[:]], dsts=[buf[:] for _ in group], alu_op=0)],
+            g.remote_dma_fused([RemoteDMATransfer(dst_ids=ids, dma_engine_mask=mask, remote_sem=arr(j, part),
+                                                  srcs=[piece], dsts=[piece for _ in group], alu_op=0)],
                                local_sem=sem.sent)
         left += _bits(mask)
 
@@ -130,6 +136,8 @@ def rank_program(g, core, T, topo):
                       start=True, stop=True).then_inc(sem["m%d" % t], 1)
             ve.wait_ge(sem["m%d" % t], 1)
             ve.tensor_tensor(T["s%d" % t][:], bank[:, 0:W], T.zero[:], AluOpType.max).then_inc(sem["r%d" % t], 1)
+        if due[rank][j][2] == 2:
+            te.wait_ge(arr(j, 2), due[rank][j][1])
         for h in range(P):
             t = i * P + h
             te.wait_ge(sem["r%d" % t], 1)

@@ -5,10 +5,10 @@ WB = 3
 SLOTS = WB + 1
 KP = 128
 QP = 512
-P = 2
+P = 4
 W = QP // P
 NS = 8 - P
-ST = 2
+ST = 4
 
 SCRATCH = {
     "qs": ("sbuf", [128, QP], "bfloat16"),
@@ -24,7 +24,7 @@ for _h in range(P):
 for _b in range(NS):
     SCRATCH["p%d" % _b] = ("psum", [128, 512], "float32")
 
-SEMAPHORES = (["kvl", "ql", "zs", "sent", "st"] + ["a%d" % s for s in range(SLOTS)] + ["b%d" % s for s in range(SLOTS)]
+SEMAPHORES = (["kl", "vl", "ql", "zs", "sent", "st"] + ["a%d" % s for s in range(SLOTS)] + ["b%d" % s for s in range(SLOTS)]
               + ["m%d" % t for t in range(SLOTS * P)] + ["r%d" % t for t in range(SLOTS * P)]
               + ["f%d" % h for h in range(P)] + ["c%d" % h for h in range(P)])
 
@@ -35,28 +35,55 @@ def _bits(m):
 
 def _plan(cores, topo):
     n = len(cores)
+
+    def cross(a, b):
+        return topo.rack(topo.host(cores[a])) != topo.rack(topo.host(cores[b]))
+
+    def room(m, j):
+        return m - WB <= j <= m or (j % SLOTS) not in [x % SLOTS for x in range(max(0, m - WB), m + 1)]
+
     first = [[] for _ in range(n)]
     rest = [[] for _ in range(n)]
     relay = [[] for _ in range(n)]
+    want = [list(range(j + 1, min(j + WB, n - 1) + 1)) for j in range(n)]
+    direct = [[r for r in want[j] if topo.may_write(cores[j], cores[r])] for j in range(n)]
+    xing = [sum(1 for r in direct[j] if cross(j, r)) for j in range(n)]
     for j in range(n):
-        dests = list(range(j + 1, min(j + WB, n - 1) + 1))
-        direct = [r for r in dests if topo.may_write(cores[j], cores[r])]
-        for r in dests:
-            if r in direct:
+        for r in want[j]:
+            if r in direct[j]:
                 continue
-            cands = [m for m in direct if topo.may_write(cores[m], cores[r])]
-            m = min(cands, key=lambda x: (x >= n - 1, len(relay[x]), x))
+            cands = [m for m in range(n) if m != j and m != r and direct[m] and room(m, j)
+                     and topo.may_write(cores[j], cores[m]) and topo.may_write(cores[m], cores[r])]
+
+            def more(m):
+                return (1 if m not in direct[j] and m not in first[j] and cross(j, m) else 0, 1 if cross(m, r) else 0)
+
+            m = min(cands, key=lambda x: (max(xing[j] + more(x)[0], xing[x] + more(x)[1]), x not in direct[j],
+                                          len(relay[x]), x))
+            xing[j] += more(m)[0]
+            xing[m] += more(m)[1]
             relay[m].append((j, r))
             if m not in first[j]:
                 first[j].append(m)
-        rest[j] = [r for r in direct if r not in first[j]]
+        rest[j] = [r for r in direct[j] if r not in first[j]]
     calls = [[] for _ in range(n)]
     due = [{r: (0, 0, 1)} for r in range(n)]
+    total = [len(first[m]) + len(rest[m]) + len(relay[m]) for m in range(n)]
+    line = [[0, 0] for _ in range(n)]
 
     def add(m, j, group, stage):
         mask = topo.mask(cores[m], cores[group[0]])
         for r in group[1:]:
             mask &= topo.mask(cores[m], cores[r])
+        if total[m] > 1:
+            eng = [e for e in range(mask.bit_length()) if (mask >> e) & 1]
+            if stage == 3:
+                side = 0 if line[m][0] < line[m][1] else 1
+            else:
+                side = 0 if cross(m, group[0]) else 1
+            line[m][side] += len(group)
+            eng = eng[:len(eng) // 2] if side == 0 else eng[len(eng) // 2:]
+            mask = sum(1 << e for e in eng)
         parts = 1 if stage == 2 else 2
         if parts == 1:
             calls[m].append((j, group, mask, 0))
@@ -69,8 +96,10 @@ def _plan(cores, topo):
     for j in range(n):
         for r in first[j]:
             add(j, j, [r], 1)
-        if rest[j]:
-            add(j, j, rest[j], 2)
+        for far in (True, False):
+            group = [r for r in rest[j] if cross(j, r) == far]
+            if group:
+                add(j, j, group, 2)
     for m in range(n):
         for j, r in relay[m]:
             add(m, j, [r], 3)
@@ -93,16 +122,19 @@ def rank_program(g, core, T, topo):
         return sem[("b%d" if part == 2 else "a%d") % (j % SLOTS)]
 
     mine = slot(rank)
-    g.sync.dma_start(mine[:, 0:KP], T.k[:]).then_inc(sem.kvl, 16)
-    g.scalar.dma_start(mine[:, KP:2 * KP], T.v[:]).then_inc(sem.kvl, 16)
+    g.sync.dma_start(mine[:, 0:KP], T.k[:]).then_inc(sem.kl, 16)
+    g.scalar.dma_start(mine[:, KP:2 * KP], T.v[:]).then_inc(sem.vl, 16)
     g.sync.dma_start(T.qs[:], T.q[:]).then_inc(sem.ql, 16)
     ve.memset(T.zero[:], 0.0).then_inc(sem.zs, 1)
 
     left = 0
-    if calls[rank]:
-        g.wait_ge(sem.kvl, 32)
     for j, group, mask, part in calls[rank]:
-        if j != rank:
+        if j == rank:
+            if part != 2:
+                g.wait_ge(sem.kl, 16)
+            if part != 1:
+                g.wait_ge(sem.vl, 16)
+        else:
             g.wait_ge(arr(j, part), due[rank][j][1])
         lo, hi = [(0, 2 * KP), (0, KP), (KP, 2 * KP)][part]
         piece = slot(j)[:, lo:hi]
@@ -119,14 +151,14 @@ def rank_program(g, core, T, topo):
                                local_sem=sem.sent)
         left += _bits(mask)
 
-    order = sorted(due[rank], key=lambda j: (due[rank][j][0], rank - j))
+    order = sorted([j for j in due[rank] if rank - WB <= j <= rank], key=lambda j: (due[rank][j][0], rank - j))
     last = len(order) - 1
     te.wait_ge(sem.ql, 16)
     ve.wait_ge(sem.zs, 1)
     for i, j in enumerate(order):
         buf = slot(j)
         if j == rank:
-            te.wait_ge(sem.kvl, 32)
+            te.wait_ge(sem.kl, 16)
         else:
             te.wait_ge(arr(j), due[rank][j][1])
         for h in range(P):
@@ -136,7 +168,9 @@ def rank_program(g, core, T, topo):
                       start=True, stop=True).then_inc(sem["m%d" % t], 1)
             ve.wait_ge(sem["m%d" % t], 1)
             ve.tensor_tensor(T["s%d" % t][:], bank[:, 0:W], T.zero[:], AluOpType.max).then_inc(sem["r%d" % t], 1)
-        if due[rank][j][2] == 2:
+        if j == rank:
+            te.wait_ge(sem.vl, 16)
+        elif due[rank][j][2] == 2:
             te.wait_ge(arr(j, 2), due[rank][j][1])
         for h in range(P):
             t = i * P + h

@@ -17,6 +17,8 @@ SCRATCH = {
 }
 for _s in range(SLOTS):
     SCRATCH["kv%d" % _s] = ("sbuf", [128, 2 * KP], "bfloat16")
+    SCRATCH["dk%d" % _s] = ("dram", [128, KP], "bfloat16")
+    SCRATCH["dv%d" % _s] = ("dram", [128, KP], "bfloat16")
 for _t in range(SLOTS * P):
     SCRATCH["s%d" % _t] = ("sbuf", [128, W], "bfloat16")
 for _h in range(P):
@@ -24,7 +26,8 @@ for _h in range(P):
 for _b in range(NS):
     SCRATCH["p%d" % _b] = ("psum", [128, 512], "float32")
 
-SEMAPHORES = (["kl", "vl", "ql", "zs", "sent", "st"] + ["a%d" % s for s in range(SLOTS)] + ["b%d" % s for s in range(SLOTS)]
+SEMAPHORES = (["kl", "vl", "ql", "kd", "vd", "zs", "sent", "st"]
+              + ["a%d" % s for s in range(SLOTS)] + ["b%d" % s for s in range(SLOTS)]
               + ["m%d" % t for t in range(SLOTS * P)] + ["r%d" % t for t in range(SLOTS * P)]
               + ["f%d" % h for h in range(P)] + ["c%d" % h for h in range(P)])
 
@@ -67,42 +70,45 @@ def _plan(cores, topo):
                 first[j].append(m)
         rest[j] = [r for r in direct[j] if r not in first[j]]
     calls = [[] for _ in range(n)]
-    due = [{r: (0, 0, 1)} for r in range(n)]
+    due = [{r: (0, 0, 0, 0, 1)} for r in range(n)]
     total = [len(first[m]) + len(rest[m]) + len(relay[m]) for m in range(n)]
     line = [[0, 0] for _ in range(n)]
 
-    def add(m, j, group, stage):
-        mask = topo.mask(cores[m], cores[group[0]])
-        for r in group[1:]:
-            mask &= topo.mask(cores[m], cores[r])
+    def add(m, j, r, passed):
+        whole = topo.mask(cores[m], cores[r])
+        mask, place = whole, 0
         if total[m] > 1:
-            eng = [e for e in range(mask.bit_length()) if (mask >> e) & 1]
-            if stage == 3:
+            eng = [e for e in range(whole.bit_length()) if (whole >> e) & 1]
+            if passed:
                 side = 0 if line[m][0] < line[m][1] else 1
             else:
-                side = 0 if cross(m, group[0]) else 1
-            line[m][side] += len(group)
+                side = 0 if cross(m, r) else 1
+            place = line[m][side]
+            line[m][side] += 1
             eng = eng[:len(eng) // 2] if side == 0 else eng[len(eng) // 2:]
             mask = sum(1 << e for e in eng)
-        parts = 1 if stage == 2 else 2
-        if parts == 1:
-            calls[m].append((j, group, mask, 0))
+        src = "d" if (m != j and m not in want[j]) or (m == j and r not in want[j]) else "s"
+        dst = "d" if r not in want[j] else "s"
+        kind = 3 if passed else 2 if cross(m, r) else 1
+        if passed or r in first[j] or cross(m, r):
+            vmask = whole if passed else mask
+            calls[m].append((j, r, mask, 1, src, dst))
+            calls[m].append((j, r, vmask, 2, src, dst))
+            due[r][j] = (kind, place, _bits(mask), _bits(vmask), 2)
         else:
-            calls[m].append((j, group, mask, 1))
-            calls[m].append((j, group, mask, 2))
-        for r in group:
-            due[r][j] = (stage, _bits(mask), parts)
+            calls[m].append((j, r, mask, 0, src, dst))
+            due[r][j] = (kind, place, _bits(mask), 0, 1)
 
     for j in range(n):
         for r in first[j]:
-            add(j, j, [r], 1)
+            add(j, j, r, False)
         for far in (True, False):
-            group = [r for r in rest[j] if cross(j, r) == far]
-            if group:
-                add(j, j, group, 2)
+            for r in rest[j]:
+                if cross(j, r) == far:
+                    add(j, j, r, False)
     for m in range(n):
         for j, r in relay[m]:
-            add(m, j, [r], 3)
+            add(m, j, r, True)
     return calls, due
 
 
@@ -121,63 +127,77 @@ def rank_program(g, core, T, topo):
     def arr(j, part=0):
         return sem[("b%d" if part == 2 else "a%d") % (j % SLOTS)]
 
+    def side(j, part, where):
+        if where == "d":
+            return T[("dv%d" if part == 2 else "dk%d") % (j % SLOTS)][:]
+        lo, hi = [(0, 2 * KP), (0, KP), (KP, 2 * KP)][part]
+        return slot(j)[:, lo:hi]
+
     mine = slot(rank)
+    flat = any(j == rank and src == "d" for j, r, mask, part, src, dst in calls[rank])
+    if flat:
+        g.sync.dma_start(side(rank, 1, "d"), T.k[:]).then_inc(sem.kd, 16)
+        g.scalar.dma_start(side(rank, 2, "d"), T.v[:]).then_inc(sem.vd, 16)
     g.sync.dma_start(mine[:, 0:KP], T.k[:]).then_inc(sem.kl, 16)
     g.scalar.dma_start(mine[:, KP:2 * KP], T.v[:]).then_inc(sem.vl, 16)
     g.sync.dma_start(T.qs[:], T.q[:]).then_inc(sem.ql, 16)
     ve.memset(T.zero[:], 0.0).then_inc(sem.zs, 1)
 
     left = 0
-    for j, group, mask, part in calls[rank]:
+    for j, r, mask, part, src, dst in calls[rank]:
         if j == rank:
             if part != 2:
-                g.wait_ge(sem.kl, 16)
+                g.wait_ge(sem.kd if src == "d" else sem.kl, 16)
             if part != 1:
-                g.wait_ge(sem.vl, 16)
+                g.wait_ge(sem.vd if src == "d" else sem.vl, 16)
         else:
-            g.wait_ge(arr(j, part), due[rank][j][1])
-        lo, hi = [(0, 2 * KP), (0, KP), (KP, 2 * KP)][part]
-        piece = slot(j)[:, lo:hi]
-        if len(group) == 1:
-            rid, pid = topo.addr(cores[group[0]], core)
-            g.remote_dma(piece, piece, arr(j, part), sem.sent, pid, rid, mask)
-        else:
-            ids = []
-            for r in group:
-                rid, pid = topo.addr(cores[r], core)
-                ids.append(DstId(rid=rid, pnc=pid))
-            g.remote_dma_fused([RemoteDMATransfer(dst_ids=ids, dma_engine_mask=mask, remote_sem=arr(j, part),
-                                                  srcs=[piece], dsts=[piece for _ in group], alu_op=0)],
-                               local_sem=sem.sent)
+            g.wait_ge(arr(j, part), due[rank][j][3 if part == 2 else 2])
+        rid, pid = topo.addr(cores[r], core)
+        g.remote_dma(side(j, part, dst), side(j, part, src), arr(j, part), sem.sent, pid, rid, mask)
         left += _bits(mask)
 
-    order = sorted([j for j in due[rank] if rank - WB <= j <= rank], key=lambda j: (due[rank][j][0], rank - j))
-    last = len(order) - 1
+    order = sorted([j for j in due[rank] if rank - WB <= j <= rank], key=lambda j: (due[rank][j][0:2], rank - j))
+    steps = []
+    late = [j for j in order if due[rank][j][4] == 2]
+    for j in order:
+        if j not in late:
+            steps += [("kq", j), ("vs", j)]
+    steps += [("kq", j) for j in late] + [("vs", j) for j in late]
+    nth = {}
+    done = 0
     te.wait_ge(sem.ql, 16)
     ve.wait_ge(sem.zs, 1)
-    for i, j in enumerate(order):
+    for what, j in steps:
         buf = slot(j)
-        if j == rank:
-            te.wait_ge(sem.kl, 16)
+        if what == "kq":
+            i = len(nth)
+            nth[j] = i
+            if j == rank:
+                te.wait_ge(sem.kl, 16)
+            else:
+                te.wait_ge(arr(j), due[rank][j][2])
+            for h in range(P):
+                t = i * P + h
+                bank = T["p%d" % (t % NS)]
+                if t >= NS:
+                    te.wait_ge(sem["r%d" % (t - NS)], 1)
+                te.matmul(bank[:, 0:W], buf[:, 0:KP], T.qs[:, h * W:(h + 1) * W],
+                          start=True, stop=True).then_inc(sem["m%d" % t], 1)
+                ve.wait_ge(sem["m%d" % t], 1)
+                ve.tensor_tensor(T["s%d" % t][:], bank[:, 0:W], T.zero[:], AluOpType.max).then_inc(sem["r%d" % t], 1)
         else:
-            te.wait_ge(arr(j), due[rank][j][1])
-        for h in range(P):
-            t = i * P + h
-            bank = T["p%d" % (t % NS)]
-            te.matmul(bank[:, 0:W], buf[:, 0:KP], T.qs[:, h * W:(h + 1) * W],
-                      start=True, stop=True).then_inc(sem["m%d" % t], 1)
-            ve.wait_ge(sem["m%d" % t], 1)
-            ve.tensor_tensor(T["s%d" % t][:], bank[:, 0:W], T.zero[:], AluOpType.max).then_inc(sem["r%d" % t], 1)
-        if j == rank:
-            te.wait_ge(sem.vl, 16)
-        elif due[rank][j][2] == 2:
-            te.wait_ge(arr(j, 2), due[rank][j][1])
-        for h in range(P):
-            t = i * P + h
-            te.wait_ge(sem["r%d" % t], 1)
-            mm = te.matmul(T["o%d" % h][:, 0:W], buf[:, KP:2 * KP], T["s%d" % t][:], start=(i == 0), stop=(i == last))
-            if i == last:
-                mm.then_inc(sem["f%d" % h], 1)
+            if j == rank:
+                te.wait_ge(sem.vl, 16)
+            elif due[rank][j][4] == 2:
+                te.wait_ge(arr(j, 2), due[rank][j][3])
+            done += 1
+            for h in range(P):
+                t = nth[j] * P + h
+                te.wait_ge(sem["r%d" % t], 1)
+                mm = te.matmul(T["o%d" % h][:, 0:W], buf[:, KP:2 * KP], T["s%d" % t][:],
+                               start=(done == 1), stop=(done == len(order)))
+                if done == len(order):
+                    mm.then_inc(sem["f%d" % h], 1)
     for h in range(P):
         ve.wait_ge(sem["f%d" % h], 1)
         ve.tensor_copy(T.ys[:, h * W:(h + 1) * W], T["o%d" % h][:, 0:W]).then_inc(sem["c%d" % h], 1)

from concourse.bass import DstId, RemoteDMATransfer
from concourse.mybir import AluOpType

WB = 3
SLOTS = WB + 1
KP = 128
QP = 512
P = 4
W = QP // P
NS = 8 - P
ST = 4

SCRATCH = {
    "qs": ("sbuf", [128, QP], "bfloat16"),
    "zero": ("sbuf", [128, W], "float32"),
    "ys": ("sbuf", [128, QP], "bfloat16"),
}
for _s in range(SLOTS):
    SCRATCH["kv%d" % _s] = ("sbuf", [128, 2 * KP], "bfloat16")
    SCRATCH["dk%d" % _s] = ("dram", [128, KP], "bfloat16")
    SCRATCH["dv%d" % _s] = ("dram", [128, KP], "bfloat16")
for _t in range(SLOTS * P):
    SCRATCH["s%d" % _t] = ("sbuf", [128, W], "bfloat16")
for _h in range(P):
    SCRATCH["o%d" % _h] = ("psum", [128, 512], "float32")
for _b in range(NS):
    SCRATCH["p%d" % _b] = ("psum", [128, 512], "float32")

SEMAPHORES = (["kl", "vl", "ql", "kd", "vd", "zs", "sent", "st"]
              + ["a%d" % s for s in range(SLOTS)] + ["b%d" % s for s in range(SLOTS)]
              + ["m%d" % t for t in range(SLOTS * P)] + ["r%d" % t for t in range(SLOTS * P)]
              + ["f%d" % h for h in range(P)] + ["c%d" % h for h in range(P)])


def _bits(m):
    return bin(m).count("1")


def _plan(cores, topo):
    n = len(cores)

    def cross(a, b):
        return topo.rack(topo.host(cores[a])) != topo.rack(topo.host(cores[b]))

    def room(m, j):
        return m - WB <= j <= m or (j % SLOTS) not in [x % SLOTS for x in range(max(0, m - WB), m + 1)]

    first = [[] for _ in range(n)]
    rest = [[] for _ in range(n)]
    relay = [[] for _ in range(n)]
    want = [list(range(j + 1, min(j + WB, n - 1) + 1)) for j in range(n)]
    direct = [[r for r in want[j] if topo.may_write(cores[j], cores[r])] for j in range(n)]
    xing = [sum(1 for r in direct[j] if cross(j, r)) for j in range(n)]
    for j in range(n):
        for r in want[j]:
            if r in direct[j]:
                continue
            cands = [m for m in range(n) if m != j and m != r and direct[m] and room(m, j)
                     and topo.may_write(cores[j], cores[m]) and topo.may_write(cores[m], cores[r])]

            def more(m):
                return (1 if m not in direct[j] and m not in first[j] and cross(j, m) else 0, 1 if cross(m, r) else 0)

            m = min(cands, key=lambda x: (max(xing[j] + more(x)[0], xing[x] + more(x)[1]), x not in direct[j],
                                          len(relay[x]), x))
            xing[j] += more(m)[0]
            xing[m] += more(m)[1]
            relay[m].append((j, r))
            if m not in first[j]:
                first[j].append(m)
        rest[j] = [r for r in direct[j] if r not in first[j]]
    calls = [[] for _ in range(n)]
    due = [{r: (0, 0, 0, 0, 1)} for r in range(n)]
    total = [len(first[m]) + len(rest[m]) + len(relay[m]) for m in range(n)]
    line = [[0, 0] for _ in range(n)]

    def add(m, j, r, passed):
        whole = topo.mask(cores[m], cores[r])
        mask, place = whole, 0
        if total[m] > 1:
            eng = [e for e in range(whole.bit_length()) if (whole >> e) & 1]
            if passed:
                side = 0 if line[m][0] < line[m][1] else 1
            else:
                side = 0 if cross(m, r) else 1
            place = line[m][side]
            line[m][side] += 1
            eng = eng[:len(eng) // 2] if side == 0 else eng[len(eng) // 2:]
            mask = sum(1 << e for e in eng)
        src = "d" if (m != j and m not in want[j]) or (m == j and r not in want[j]) else "s"
        dst = "d" if r not in want[j] else "s"
        kind = 3 if passed else 2 if cross(m, r) else 1
        if passed or r in first[j] or cross(m, r):
            vmask = whole if passed else mask
            calls[m].append((j, r, mask, 1, src, dst))
            calls[m].append((j, r, vmask, 2, src, dst))
            due[r][j] = (kind, place, _bits(mask), _bits(vmask), 2)
        else:
            calls[m].append((j, r, mask, 0, src, dst))
            due[r][j] = (kind, place, _bits(mask), 0, 1)

    for j in range(n):
        for r in first[j]:
            add(j, j, r, False)
        for far in (True, False):
            for r in rest[j]:
                if cross(j, r) == far:
                    add(j, j, r, False)
    for m in range(n):
        for j, r in relay[m]:
            add(m, j, r, True)
    return calls, due


def rank_program(g, core, T, topo):
    rank = T.rank_of(core)
    if rank is None:
        return
    cores = list(T.cores)
    calls, due = _plan(cores, topo)
    sem = T.sem
    te, ve = g.tensor, g.vector

    def slot(j):
        return T["kv%d" % (j % SLOTS)]

    def arr(j, part=0):
        return sem[("b%d" if part == 2 else "a%d") % (j % SLOTS)]

    def side(j, part, where):
        if where == "d":
            return T[("dv%d" if part == 2 else "dk%d") % (j % SLOTS)][:]
        lo, hi = [(0, 2 * KP), (0, KP), (KP, 2 * KP)][part]
        return slot(j)[:, lo:hi]

    mine = slot(rank)
    flat = any(j == rank and src == "d" for j, r, mask, part, src, dst in calls[rank])
    if flat:
        g.sync.dma_start(side(rank, 1, "d"), T.k[:]).then_inc(sem.kd, 16)
        g.scalar.dma_start(side(rank, 2, "d"), T.v[:]).then_inc(sem.vd, 16)
    g.sync.dma_start(mine[:, 0:KP], T.k[:]).then_inc(sem.kl, 16)
    g.scalar.dma_start(mine[:, KP:2 * KP], T.v[:]).then_inc(sem.vl, 16)
    g.sync.dma_start(T.qs[:], T.q[:]).then_inc(sem.ql, 16)
    ve.memset(T.zero[:], 0.0).then_inc(sem.zs, 1)

    left = 0
    for j, r, mask, part, src, dst in calls[rank]:
        if j == rank:
            if part != 2:
                g.wait_ge(sem.kd if src == "d" else sem.kl, 16)
            if part != 1:
                g.wait_ge(sem.vd if src == "d" else sem.vl, 16)
        else:
            g.wait_ge(arr(j, part), due[rank][j][3 if part == 2 else 2])
        rid, pid = topo.addr(cores[r], core)
        g.remote_dma(side(j, part, dst), side(j, part, src), arr(j, part), sem.sent, pid, rid, mask)
        left += _bits(mask)

    order = sorted([j for j in due[rank] if rank - WB <= j <= rank], key=lambda j: (due[rank][j][0:2], rank - j))
    steps = []
    late = [j for j in order if due[rank][j][4] == 2]
    for j in order:
        if j not in late:
            steps += [("kq", j), ("vs", j)]
    steps += [("kq", j) for j in late] + [("vs", j) for j in late]
    nth = {}
    done = 0
    te.wait_ge(sem.ql, 16)
    ve.wait_ge(sem.zs, 1)
    for what, j in steps:
        buf = slot(j)
        if what == "kq":
            i = len(nth)
            nth[j] = i
            if j == rank:
                te.wait_ge(sem.kl, 16)
            else:
                te.wait_ge(arr(j), due[rank][j][2])
            for h in range(P):
                t = i * P + h
                bank = T["p%d" % (t % NS)]
                if t >= NS:
                    te.wait_ge(sem["r%d" % (t - NS)], 1)
                te.matmul(bank[:, 0:W], buf[:, 0:KP], T.qs[:, h * W:(h + 1) * W],
                          start=True, stop=True).then_inc(sem["m%d" % t], 1)
                ve.wait_ge(sem["m%d" % t], 1)
                ve.tensor_tensor(T["s%d" % t][:], bank[:, 0:W], T.zero[:], AluOpType.max).then_inc(sem["r%d" % t], 1)
        else:
            if j == rank:
                te.wait_ge(sem.vl, 16)
            elif due[rank][j][4] == 2:
                te.wait_ge(arr(j, 2), due[rank][j][3])
            done += 1
            for h in range(P):
                t = nth[j] * P + h
                te.wait_ge(sem["r%d" % t], 1)
                mm = te.matmul(T["o%d" % h][:, 0:W], buf[:, KP:2 * KP], T["s%d" % t][:],
                               start=(done == 1), stop=(done == len(order)))
                if done == len(order):
                    mm.then_inc(sem["f%d" % h], 1)
    for h in range(P):
        ve.wait_ge(sem["f%d" % h], 1)
        ve.tensor_copy(T.ys[:, h * W:(h + 1) * W], T["o%d" % h][:, 0:W]).then_inc(sem["c%d" % h], 1)

    queues = [g.sync, g.scalar]
    per = P // ST
    for s in range(ST):
        qu = queues[s % 2]
        for h in range(s * per, (s + 1) * per):
            qu.wait_ge(sem["c%d" % h], 1)
        lo, hi = s * per * W, (s + 1) * per * W
        qu.dma_start(T.y[:, lo:hi], T.ys[:, lo:hi]).then_inc(sem.st, 16)

    if left:
        g.wait_ge(sem.sent, left)
    g.wait_ge(sem.st, 16 * ST)
